import numpy as np
import ml_dtypes


def mxq(x, axis, fmt="e4m3"):
    dtype, down = {"e4m3": (ml_dtypes.float8_e4m3fn, 7), "e5m2": (ml_dtypes.float8_e5m2, 14)}[fmt]
    v = np.moveaxis(np.asarray(x, np.float32).astype(ml_dtypes.bfloat16).astype(np.float64), axis, -1)
    blocks = v.reshape(v.shape[:-1] + (-1, 32))
    amax = np.abs(blocks).max(-1, keepdims=True)
    byte = np.maximum(np.where(amax > 0, np.frexp(amax)[1] - 1 + 127, 0) - down, 1)
    scale = np.exp2(byte - 127.0)
    codes = (blocks / scale).astype(np.float32).astype(dtype).astype(np.float64)
    return np.moveaxis((codes * scale).reshape(v.shape), -1, axis)


WIDE = False


def mx_kscale(k):
    if not WIDE:
        return np.ones(k)
    levels = np.array([10, -10, 5, -5, 0])
    if k % 512:
        return np.exp2(np.random.permutation(np.resize(levels, k // 32))).repeat(32)
    a = np.empty((k // 512, 16))
    for p in range(k // 512):
        a[p, :8] = np.random.permutation(np.resize(levels, 8))
        for g in range(8):
            far = levels[np.abs(levels - a[p, g]) >= 10]
            a[p, g + 8] = far[np.random.randint(len(far))]
    return np.exp2(a.ravel()).repeat(32)


def f64(x):
    return np.asarray(x).astype(np.float64)


def striped(idx):
    return np.tile(idx.reshape(-1, 16).T, (8, 1)).astype(np.uint16)


def unstriped(offs):
    return offs[:16].T.reshape(-1).astype(np.int64)


def pack_weight(w):
    k, n = w.shape
    w = f64(np.asarray(w, np.float32).astype(ml_dtypes.bfloat16)).reshape(k // 32, 32, n)
    amax = np.abs(w).max(1)
    byte = np.clip(np.where(amax > 0, np.frexp(amax)[1] - 1 + 127 - 7, 1), 1, 254)
    scaled = (w * np.exp2(127.0 - byte)[:, None, :]).reshape(k, n).astype(np.float32)
    words = np.ascontiguousarray(scaled.reshape(k // 512, 128, 4, n).transpose(0, 1, 3, 2)).astype(ml_dtypes.float8_e4m3fn).view(np.uint8)
    return words, np.ascontiguousarray(byte.astype(np.uint8).reshape(k // 512, 16, n))


def unpack_weight(words, scales):
    g, p, n, _ = words.shape
    vals = np.ascontiguousarray(words).view(ml_dtypes.float8_e4m3fn).astype(np.float64) * np.repeat(np.exp2(scales.astype(np.float64) - 127.0), 8, axis=1)[..., None]
    return vals.transpose(0, 1, 3, 2).reshape(g * 512, n)


E2M1 = np.array([0.0, 0.5, 1.0, 1.5, 2.0, 3.0, 4.0, 6.0, -0.0, -0.5, -1.0, -1.5, -2.0, -3.0, -4.0, -6.0])


def pack_fp4(w):
    k, n = w.shape
    w = f64(np.asarray(w, np.float32).astype(ml_dtypes.bfloat16)).reshape(k // 32, 32, n)
    amax = np.abs(w).max(1)
    mant, ex = np.frexp(amax / 6.0)
    byte = np.clip(np.where(amax > 0, np.where(mant > 0.5, ex, ex - 1) + 127, 1), 1, 254)
    scaled = (w * np.exp2(127.0 - byte)[:, None, :]).reshape(k, n).astype(np.float32)
    c = np.ascontiguousarray(scaled.reshape(k // 512, 128, 4, n).transpose(0, 1, 3, 2)).astype(ml_dtypes.float4_e2m1fn).view(np.uint8) & 0xF
    words = (c[..., 0::2] | (c[..., 1::2] << 4)).reshape(k // 512, 128, 2 * n)
    return np.ascontiguousarray(words), np.ascontiguousarray(byte.astype(np.uint8).reshape(k // 512, 16, n))


def unpack_fp4(words, scales):
    g, _, n = scales.shape
    words = np.ascontiguousarray(words).reshape(g, 128, n, 2)
    nib = np.empty((g, 128, n, 4), np.uint8)
    nib[..., 0::2] = words & 0xF
    nib[..., 1::2] = words >> 4
    vals = E2M1[nib] * np.repeat(np.exp2(scales.astype(np.float64) - 127.0), 8, axis=1)[..., None]
    return vals.transpose(0, 1, 3, 2).reshape(g * 512, n)


def relu(v):
    return np.maximum(v, 0.0)


K, T, S, H, N, U = 1024, 2048, 512, 512, 128, 1024


def setup_inputs():
    n = np.random.standard_normal
    s = mx_kscale(K)[:, None]
    u = mx_kscale(H)
    packed_xT = pack_weight(n((K, T)) * s)
    packed_w2 = pack_fp4(n((H, N)) / np.sqrt(H) / u[:, None])
    return {
        "x_words": packed_xT[0],
        "x_scales": packed_xT[1],
        "w1": (n((K, H)) / np.sqrt(K) / s * u).astype(np.float32),
        "w2_words": packed_w2[0],
        "w2_scales": packed_w2[1],
        "skip": (n((H, U)) * u[:, None]).astype(np.float32),
        "offs": striped(np.random.permutation(T)[:S]),
        "cell": striped(np.random.permutation(U)[:S]),
    }


def reference(x_words, x_scales, w1, w2_words, w2_scales, skip, offs, cell):
    xq = unpack_weight(x_words, x_scales)[:, unstriped(offs)]
    up = np.zeros((H, U))
    up[:, unstriped(cell)] = relu(mxq(f64(w1), 0, "e4m3").T @ xq)
    z = up + f64(skip)
    return unpack_fp4(w2_words, w2_scales).T @ mxq(z, 0, "e4m3")

@@ -1,0 +1,222 @@
+from contextlib import ExitStack
+
+import concourse.mybir as mybir
+from concourse.masks import make_identity
+
+K, T, S, H, N, U = 1024, 2048, 512, 512, 128, 1024
+FLOPS = 2 * K * H * S + 2 * H * N * U
+
+F32 = mybir.dt.float32
+BF16 = mybir.dt.bfloat16
+I32 = mybir.dt.int32
+U32 = mybir.dt.uint32
+U16 = mybir.dt.uint16
+U8 = mybir.dt.uint8
+FP8X4 = mybir.dt.float8_e4m3fn_x4
+FP4X4 = mybir.dt.float4_e2m1fn_x4
+RELU = mybir.ActivationFunctionType.Relu
+COPY = mybir.ActivationFunctionType.Copy
+
+P = 128
+PACK = 4
+K_PASS = P * PACK
+PASSES = K // K_PASS
+HALF = S // 2
+QUARTER = U // 4
+FIRST = 256
+
+
+def tile_picked_unet_relu_p_kernel(tc, x_words, x_scales, w1, w2_words, w2_scales, skip, offs, cell, out):
+    nc = tc.nc
+    with ExitStack() as ctx:
+        lists = ctx.enter_context(tc.tile_pool(name="lists", bufs=1))
+        sb = ctx.enter_context(tc.tile_pool(name="sb", bufs=1))
+        psum = ctx.enter_context(tc.psum_pool(name="psum", bufs=1))
+
+        def bank(number, shape, name):
+            return psum.tile(shape, F32, name=name, tag="bank%d" % number)
+
+        def load_w1(g, c0, c1, name):
+            raw = sb.tile([P, PACK, c1 - c0], F32, name=name, tag=name)
+            nc.sync.dma_start(raw[:], w1[g * K_PASS : (g + 1) * K_PASS, c0:c1].rearrange("(p j) c -> p j c", j=PACK))
+            return raw
+
+        offs_t = lists.tile([P, S // 16], U16, name="offs_t")
+        cell_t = lists.tile([P, S // 16], U16, name="cell_t")
+        xs = sb.tile([P, T], U8, name="xs")
+        nc.gpsimd.memset(xs[:].bitcast(I32), 0)
+        nc.sync.dma_start(offs_t[:], offs)
+        xw = [sb.tile([P, T], U32, name="xw%d" % g) for g in range(PASSES)]
+        nc.sync.dma_start(xw[0][:].bitcast(I32), x_words[0].rearrange("p n t -> p (n t)").bitcast(I32))
+        for q in range(4):
+            nc.sync.dma_start(xs[32 * q : 32 * q + 8, :].bitcast(I32), x_scales[:, 4 * q : 4 * q + 4, :].bitcast(I32))
+        raw0 = [load_w1(g, 0, 128, "raw0_%d" % g) for g in range(PASSES)]
+        nc.sync.dma_start(xw[1][:].bitcast(I32), x_words[1].rearrange("p n t -> p (n t)").bitcast(I32))
+        nc.sync.dma_start(cell_t[:], cell)
+        raw1 = sb.tile([P, PASSES, PACK, P], F32, name="raw1", tag="raw1")
+        for g in range(PASSES):
+            nc.sync.dma_start(raw1[:, g], w1[g * K_PASS : (g + 1) * K_PASS, 128:256].rearrange("(p j) c -> p j c", j=PACK))
+        raw23 = [load_w1(g, 256, 512, "raw23_%d" % g) for g in range(PASSES)]
+        skip_t = [sb.tile([P, U], F32, name="skip%d" % b) for b in range(4)]
+        skip_dealt = skip[256:512, :].rearrange("(r u e) v -> u r e v", u=2, e=2)
+        skip_rows = [skip[0:128, :], skip[128:256, :], skip_dealt[0], skip_dealt[1]]
+        for b in range(4):
+            nc.sync.dma_start(skip_t[b][:], skip_rows[b])
+
+        ident = sb.tile([P, P], F32, name="ident")
+        make_identity(nc, ident[:])
+        w2c = sb.tile([P, 2 * N], U8, name="w2c", align_bytes=64)
+        w2s = sb.tile([P, N], U8, name="w2s", align_bytes=64)
+        nc.gpsimd.memset(w2s[:], 0)
+        nc.sync.dma_start(w2c[:].bitcast(I32), w2_words[0].bitcast(I32))
+        for q in range(4):
+            nc.sync.dma_start(w2s[32 * q : 32 * q + 4, :].bitcast(I32), w2_scales[0, 4 * q : 4 * q + 4, :].bitcast(I32))
+
+        up = [sb.tile([P, U], F32, name="up%d" % b, tag="up%d" % b) for b in range(4)]
+        for b in range(4):
+            nc.vector.memset(up[b][:], 0.0)
+
+        def quantise(grouped, width, name):
+            codes = sb.tile([P, width], U32, name=name + "_c", align_bytes=64)
+            scales = sb.tile([P, width], U8, name=name + "_s", align_bytes=64)
+            nc.vector.quantize_mx(out=codes[:].bitcast(FP8X4), scales=scales[:], in_=grouped)
+            return codes, scales
+
+        def w1_plain(raw, name):
+            grouped = sb.tile([P, PASSES, K_PASS], BF16, name=name, align_bytes=64)
+            for g in range(PASSES):
+                nc.scalar.activation(
+                    grouped[:, g, :].rearrange("p (c i t) -> p c t i", i=4, t=PACK),
+                    raw[g][:].rearrange("p t (c i) -> p c t i", i=4),
+                    COPY,
+                )
+            return quantise(grouped[:].rearrange("p g n -> p (g n)"), PASSES * P, name)
+
+        def w1_dealt(raw, name):
+            grouped = sb.tile([P, 2, PASSES, K_PASS], BF16, name=name, align_bytes=64)
+            for g in range(PASSES):
+                nc.scalar.copy(
+                    grouped[:, :, g, :].rearrange("p u (r e j) -> p r j u e", e=2, j=PACK),
+                    raw[g][:].rearrange("p j (r u e) -> p r j u e", u=2, e=2),
+                )
+            return quantise(grouped[:].rearrange("p u g n -> p (u g n)"), 2 * PASSES * P, name)
+
+        w0 = w1_plain(raw0, "w0")
+
+        xsg = sb.tile([P, S], U8, name="xsg", align_bytes=64)
+        nc.vector.tensor_copy(xsg[:], xs[:].indirect(offs_t[:]))
+        xg0 = sb.tile([P, S], U32, name="xg0", align_bytes=64)
+        nc.vector.tensor_copy(xg0[:], xw[0][:].indirect(offs_t[:]))
+        xg1_first = sb.tile([P, FIRST], U32, name="xg1_first", align_bytes=64)
+        nc.vector.tensor_copy(xg1_first[:], xw[1][:].indirect(offs_t[:, 0 : FIRST // 16]))
+        xg1_rest = sb.tile([P, S - FIRST], U32, name="xg1_rest", align_bytes=64)
+        nc.vector.tensor_copy(xg1_rest[:], xw[1][:].indirect(offs_t[:, FIRST // 16 : S // 16]))
+
+        def first_product(acc, j0, j1, w, col0):
+            codes, scales = w
+            cols = slice(j0, j1)
+            moving = [xg0[:, cols], xg1_first[:] if j0 == 0 else xg1_rest[:, j0 - FIRST : j1 - FIRST]]
+            for g in range(PASSES):
+                wc = slice(col0 + g * P, col0 + (g + 1) * P)
+                nc.tensor.matmul_mx(
+                    out=acc,
+                    lhsT=codes[:, wc].bitcast(FP8X4),
+                    lhsT_scale=scales[:, wc],
+                    rhs=moving[g].bitcast(FP8X4),
+                    rhs_scale=xsg[4 * g : P, cols],
+                    start=(g == 0),
+                    stop=(g == PASSES - 1),
+                )
+
+        def half_product(b, s, w, col0):
+            acc = bank(s, [P, HALF], "h%d_%d" % (b, s))
+            first_product(acc[:], s * HALF, (s + 1) * HALF, w, col0)
+            return acc
+
+        def scatter(b, values, j0, j1):
+            nc.vector.tensor_copy(up[b][:].indirect(cell_t[:, j0 // 16 : j1 // 16]), values)
+
+        def relu_scatter(b, j0, j1, acc, tag):
+            hs = sb.tile([P, j1 - j0], F32, name="hs%d_%d" % (b, j0), tag=tag)
+            nc.scalar.activation(hs[:], acc[:], RELU)
+            scatter(b, hs[:], j0, j1)
+
+        def whole_tile(b, col0):
+            hs = sb.tile([P, S], F32, name="hs%d" % b)
+            for s in range(2):
+                nc.scalar.activation(hs[:, s * HALF : (s + 1) * HALF], half_product(b, s, w23, col0)[:], RELU)
+            scatter(b, hs[:], 0, S)
+
+        zt0 = [sb.tile([P, 4, 256], BF16, name="zt0_%d" % vg, tag="zt0_%d" % vg) for vg in range(2)]
+        zt1 = [sb.tile([P, 2, 256], BF16, name="zt1_%d" % q) for q in range(4)]
+
+        def turn_and_add(b, number, vb0, count, ident_up):
+            acc = bank(number, [P, count, P], "t%d_%d" % (b, vb0))
+            for n, (src, one) in enumerate(((skip_t[b], ident), (up[b], ident_up))):
+                for vb in range(count):
+                    v0 = (vb0 + vb) * P
+                    nc.tensor.matmul(acc[:, vb, :], src[:, v0 : v0 + P], one[:], start=(n == 0 and vb == 0), stop=(n == 1 and vb == count - 1), is_transpose=True)
+            return acc
+
+        def round_plain(b, banks):
+            for vg in range(2):
+                src = turn_and_add(b, banks[vg], 4 * vg, 4, ident)[:].rearrange("p vb (r u e) -> p u vb r e", u=2, e=2)
+                nc.scalar.copy(zt0[vg][:, :, 64 * b : 64 * (b + 1)].rearrange("p vb (r e) -> p vb r e", e=2), src[:, 0])
+                for h in range(2):
+                    nc.scalar.copy(zt1[2 * vg + h][:, :, 64 * b : 64 * (b + 1)].rearrange("p vb (r e) -> p vb r e", e=2), src[:, 1, 2 * h : 2 * h + 2])
+
+        def turn_back(u, q, view):
+            for vb in range(2):
+                nc.tensor.transpose(words[q][:, u, vb * P : (vb + 1) * P], view[:, vb, :], ident[:])
+
+        relu_scatter(0, 0, HALF, half_product(0, 0, w0, 0), "hs0_0")
+        acc = half_product(0, 1, w0, 0)
+        grouped1 = sb.tile([P, PASSES, K_PASS], BF16, name="grouped1", align_bytes=64)
+        nc.scalar.copy(
+            grouped1[:].rearrange("p g (c i t) -> p g c t i", i=4, t=PACK),
+            raw1[:].rearrange("p g t (c i) -> p g c t i", i=4),
+        )
+        w1q = quantise(grouped1[:].rearrange("p g n -> p (g n)"), PASSES * P, "w1q")
+        relu_scatter(0, HALF, S, acc, "raw1")
+        relu_scatter(1, 0, HALF, half_product(1, 0, w1q, 0), "hs1_0")
+        acc = half_product(1, 1, w1q, 0)
+        w23 = w1_dealt(raw23, "w23")
+        relu_scatter(1, HALF, S, acc, "raw23_1")
+        whole_tile(2, 0)
+        whole_tile(3, PASSES * P)
+
+        round_plain(0, (2, 3))
+        round_plain(1, (4, 5))
+        for vg in range(2):
+            nc.scalar.copy(zt0[vg][:, :, 128:256], turn_and_add(2, 6 + vg, 4 * vg, 4, ident)[:])
+        words = [bank(4 + q, [P, 2, QUARTER], "words%d" % q) for q in range(4)]
+        for q in range(4):
+            turn_back(0, q, zt0[q // 2][:].bitcast(F32)[:, 2 * (q % 2) : 2 * (q % 2) + 2, :])
+
+        ident_last = sb.tile([P, P], F32, name="ident_last", tag="zt0_1")
+        nc.scalar.copy(ident_last[:], ident[:])
+        for q in range(4):
+            nc.vector.tensor_copy(zt1[q][:, :, 128:256], turn_and_add(3, q, 2 * q, 2, ident_last)[:])
+        for q in range(4):
+            turn_back(1, q, zt1[q][:].bitcast(F32))
+
+        zb = [sb.tile([P, QUARTER * PACK], BF16, name="zb%d" % q, align_bytes=64) for q in range(4)]
+        weave = [nc.scalar.copy, nc.vector.tensor_copy, nc.scalar.copy, nc.scalar.copy]
+        for q in range(4):
+            weave[q](zb[q][:].bitcast(F32).rearrange("p (v u) -> p v u", u=2), words[q][:].rearrange("p u v -> p v u"))
+        leave = [nc.scalar.copy, nc.scalar.copy, nc.scalar.copy, nc.vector.tensor_copy]
+        for q in range(4):
+            codes, scales = quantise(zb[q][:], QUARTER, "zq%d" % q)
+            acc = bank(q, [P, QUARTER], "o%d" % q)
+            nc.tensor.matmul_mx(
+                out=acc[:],
+                lhsT=w2c[:].bitcast(FP4X4),
+                lhsT_scale=w2s[:],
+                rhs=codes[:].bitcast(FP8X4),
+                rhs_scale=scales[:],
+                start=True,
+                stop=True,
+            )
+            res = sb.tile([P, QUARTER], F32, name="res%d" % q)
+            leave[q](res[:], acc[:])
+            nc.sync.dma_start(out[:, q * QUARTER : (q + 1) * QUARTER], res[:])

@@ -43,19 +43,20 @@ def tile_picked_unet_relu_p_kernel(tc, x_words, x_scales, w1, w2_words, w2_scale
 
         offs_t = lists.tile([P, S // 16], U16, name="offs_t")
         cell_t = lists.tile([P, S // 16], U16, name="cell_t")
-        xs = sb.tile([P, T], U8, name="xs")
-        nc.gpsimd.memset(xs[:].bitcast(I32), 0)
+        xs = sb.tile([P, PASSES * T], U8, name="xs")
+        nc.vector.memset(xs[:].bitcast(I32), 0)
         nc.sync.dma_start(offs_t[:], offs)
         xw = [sb.tile([P, T], U32, name="xw%d" % g) for g in range(PASSES)]
         nc.sync.dma_start(xw[0][:].bitcast(I32), x_words[0].rearrange("p n t -> p (n t)").bitcast(I32))
         for q in range(4):
-            nc.sync.dma_start(xs[32 * q : 32 * q + 8, :].bitcast(I32), x_scales[:, 4 * q : 4 * q + 4, :].bitcast(I32))
+            nc.sync.dma_start(
+                xs[32 * q : 32 * q + 4, :].bitcast(I32).rearrange("r (g n) -> r g n", g=PASSES),
+                x_scales[:, 4 * q : 4 * q + 4, :].bitcast(I32).rearrange("g r n -> r g n"),
+            )
         raw0 = [load_w1(g, 0, 128, "raw0_%d" % g) for g in range(PASSES)]
         nc.sync.dma_start(xw[1][:].bitcast(I32), x_words[1].rearrange("p n t -> p (n t)").bitcast(I32))
         nc.sync.dma_start(cell_t[:], cell)
-        raw1 = sb.tile([P, PASSES, PACK, P], F32, name="raw1", tag="raw1")
-        for g in range(PASSES):
-            nc.sync.dma_start(raw1[:, g], w1[g * K_PASS : (g + 1) * K_PASS, 128:256].rearrange("(p j) c -> p j c", j=PACK))
+        raw1 = [load_w1(g, 128, 256, "raw1_%d" % g) for g in range(PASSES)]
         raw23 = [load_w1(g, 256, 512, "raw23_%d" % g) for g in range(PASSES)]
         skip_t = [sb.tile([P, U], F32, name="skip%d" % b) for b in range(4)]
         skip_dealt = skip[256:512, :].rearrange("(r u e) v -> u r e v", u=2, e=2)
@@ -66,15 +67,16 @@ def tile_picked_unet_relu_p_kernel(tc, x_words, x_scales, w1, w2_words, w2_scale
         ident = sb.tile([P, P], F32, name="ident")
         make_identity(nc, ident[:])
         w2c = sb.tile([P, 2 * N], U8, name="w2c", align_bytes=64)
+        nc.sync.dma_start(w2c[:].bitcast(I32), w2_words[0].bitcast(I32))
         w2s = sb.tile([P, N], U8, name="w2s", align_bytes=64)
         nc.gpsimd.memset(w2s[:], 0)
-        nc.sync.dma_start(w2c[:].bitcast(I32), w2_words[0].bitcast(I32))
         for q in range(4):
             nc.sync.dma_start(w2s[32 * q : 32 * q + 4, :].bitcast(I32), w2_scales[0, 4 * q : 4 * q + 4, :].bitcast(I32))
 
         up = [sb.tile([P, U], F32, name="up%d" % b, tag="up%d" % b) for b in range(4)]
-        for b in range(4):
+        for b in range(2):
             nc.vector.memset(up[b][:], 0.0)
+            nc.scalar.activation(up[b + 2][:], up[b][:], COPY)
 
         def quantise(grouped, width, name):
             codes = sb.tile([P, width], U32, name=name + "_c", align_bytes=64)
@@ -99,12 +101,13 @@ def tile_picked_unet_relu_p_kernel(tc, x_words, x_scales, w1, w2_words, w2_scale
                     grouped[:, :, g, :].rearrange("p u (r e j) -> p r j u e", e=2, j=PACK),
                     raw[g][:].rearrange("p j (r u e) -> p r j u e", u=2, e=2),
                 )
-            return quantise(grouped[:].rearrange("p u g n -> p (u g n)"), 2 * PASSES * P, name)
+            return [quantise(grouped[:, u].rearrange("p g n -> p (g n)"), PASSES * P, "%s_%d" % (name, u)) for u in range(2)]
 
         w0 = w1_plain(raw0, "w0")
 
-        xsg = sb.tile([P, S], U8, name="xsg", align_bytes=64)
-        nc.vector.tensor_copy(xsg[:], xs[:].indirect(offs_t[:]))
+        xsg = [sb.tile([P, S], U8, name="xsg%d" % g, align_bytes=64) for g in range(PASSES)]
+        for g in range(PASSES):
+            nc.vector.tensor_copy(xsg[g][:], xs[:, g * T : (g + 1) * T].indirect(offs_t[:]))
         xg0 = sb.tile([P, S], U32, name="xg0", align_bytes=64)
         nc.vector.tensor_copy(xg0[:], xw[0][:].indirect(offs_t[:]))
         xg1_first = sb.tile([P, FIRST], U32, name="xg1_first", align_bytes=64)
@@ -123,13 +126,13 @@ def tile_picked_unet_relu_p_kernel(tc, x_words, x_scales, w1, w2_words, w2_scale
                     lhsT=codes[:, wc].bitcast(FP8X4),
                     lhsT_scale=scales[:, wc],
                     rhs=moving[g].bitcast(FP8X4),
-                    rhs_scale=xsg[4 * g : P, cols],
+                    rhs_scale=xsg[g][:, cols],
                     start=(g == 0),
                     stop=(g == PASSES - 1),
                 )
 
         def half_product(b, s, w, col0):
-            acc = bank(s, [P, HALF], "h%d_%d" % (b, s))
+            acc = bank((0, 4, 0, 2)[b] + s, [P, HALF], "h%d_%d" % (b, s))
             first_product(acc[:], s * HALF, (s + 1) * HALF, w, col0)
             return acc
 
@@ -141,10 +144,10 @@ def tile_picked_unet_relu_p_kernel(tc, x_words, x_scales, w1, w2_words, w2_scale
             nc.scalar.activation(hs[:], acc[:], RELU)
             scatter(b, hs[:], j0, j1)
 
-        def whole_tile(b, col0):
+        def whole_tile(b, w):
             hs = sb.tile([P, S], F32, name="hs%d" % b)
             for s in range(2):
-                nc.scalar.activation(hs[:, s * HALF : (s + 1) * HALF], half_product(b, s, w23, col0)[:], RELU)
+                nc.scalar.activation(hs[:, s * HALF : (s + 1) * HALF], w[s][:], RELU)
             scatter(b, hs[:], 0, S)
 
         zt0 = [sb.tile([P, 4, 256], BF16, name="zt0_%d" % vg, tag="zt0_%d" % vg) for vg in range(2)]
@@ -171,32 +174,28 @@ def tile_picked_unet_relu_p_kernel(tc, x_words, x_scales, w1, w2_words, w2_scale
 
         relu_scatter(0, 0, HALF, half_product(0, 0, w0, 0), "hs0_0")
         acc = half_product(0, 1, w0, 0)
-        grouped1 = sb.tile([P, PASSES, K_PASS], BF16, name="grouped1", align_bytes=64)
-        nc.scalar.copy(
-            grouped1[:].rearrange("p g (c i t) -> p g c t i", i=4, t=PACK),
-            raw1[:].rearrange("p g t (c i) -> p g c t i", i=4),
-        )
-        w1q = quantise(grouped1[:].rearrange("p g n -> p (g n)"), PASSES * P, "w1q")
-        relu_scatter(0, HALF, S, acc, "raw1")
+        w1q = w1_plain(raw1, "w1q")
+        relu_scatter(0, HALF, S, acc, "raw1_1")
         relu_scatter(1, 0, HALF, half_product(1, 0, w1q, 0), "hs1_0")
         acc = half_product(1, 1, w1q, 0)
         w23 = w1_dealt(raw23, "w23")
         relu_scatter(1, HALF, S, acc, "raw23_1")
-        whole_tile(2, 0)
-        whole_tile(3, PASSES * P)
+        late = [[half_product(2 + u, s, w23[u], 0) for s in range(2)] for u in range(2)]
+        whole_tile(2, late[0])
+        whole_tile(3, late[1])
 
-        round_plain(0, (2, 3))
-        round_plain(1, (4, 5))
+        round_plain(1, (0, 1))
+        round_plain(0, (4, 3))
         for vg in range(2):
             nc.scalar.copy(zt0[vg][:, :, 128:256], turn_and_add(2, 6 + vg, 4 * vg, 4, ident)[:])
         words = [bank(4 + q, [P, 2, QUARTER], "words%d" % q) for q in range(4)]
         for q in range(4):
             turn_back(0, q, zt0[q // 2][:].bitcast(F32)[:, 2 * (q % 2) : 2 * (q % 2) + 2, :])
 
-        ident_last = sb.tile([P, P], F32, name="ident_last", tag="zt0_1")
+        ident_last = sb.tile([P, P], F32, name="ident_last", tag="zt0_0")
         nc.scalar.copy(ident_last[:], ident[:])
         for q in range(4):
-            nc.vector.tensor_copy(zt1[q][:, :, 128:256], turn_and_add(3, q, 2 * q, 2, ident_last)[:])
+            (nc.vector.tensor_copy, nc.scalar.copy)[q % 2](zt1[q][:, :, 128:256], turn_and_add(3, q, 2 * q, 2, ident_last)[:])
         for q in range(4):
             turn_back(1, q, zt1[q][:].bitcast(F32))
 

from contextlib import ExitStack

import concourse.mybir as mybir
from concourse.masks import make_identity

K, T, S, H, N, U = 1024, 2048, 512, 512, 128, 1024
FLOPS = 2 * K * H * S + 2 * H * N * U

F32 = mybir.dt.float32
BF16 = mybir.dt.bfloat16
I32 = mybir.dt.int32
U32 = mybir.dt.uint32
U16 = mybir.dt.uint16
U8 = mybir.dt.uint8
FP8X4 = mybir.dt.float8_e4m3fn_x4
FP4X4 = mybir.dt.float4_e2m1fn_x4
RELU = mybir.ActivationFunctionType.Relu
COPY = mybir.ActivationFunctionType.Copy

P = 128
PACK = 4
K_PASS = P * PACK
PASSES = K // K_PASS
HALF = S // 2
QUARTER = U // 4
FIRST = 256


def tile_picked_unet_relu_p_kernel(tc, x_words, x_scales, w1, w2_words, w2_scales, skip, offs, cell, out):
    nc = tc.nc
    with ExitStack() as ctx:
        lists = ctx.enter_context(tc.tile_pool(name="lists", bufs=1))
        sb = ctx.enter_context(tc.tile_pool(name="sb", bufs=1))
        psum = ctx.enter_context(tc.psum_pool(name="psum", bufs=1))

        def bank(number, shape, name):
            return psum.tile(shape, F32, name=name, tag="bank%d" % number)

        def load_w1(g, c0, c1, name):
            raw = sb.tile([P, PACK, c1 - c0], F32, name=name, tag=name)
            nc.sync.dma_start(raw[:], w1[g * K_PASS : (g + 1) * K_PASS, c0:c1].rearrange("(p j) c -> p j c", j=PACK))
            return raw

        offs_t = lists.tile([P, S // 16], U16, name="offs_t")
        cell_t = lists.tile([P, S // 16], U16, name="cell_t")
        xs = sb.tile([P, PASSES * T], U8, name="xs")
        nc.vector.memset(xs[:].bitcast(I32), 0)
        nc.sync.dma_start(offs_t[:], offs)
        xw = [sb.tile([P, T], U32, name="xw%d" % g) for g in range(PASSES)]
        nc.sync.dma_start(xw[0][:].bitcast(I32), x_words[0].rearrange("p n t -> p (n t)").bitcast(I32))
        for q in range(4):
            nc.sync.dma_start(
                xs[32 * q : 32 * q + 4, :].bitcast(I32).rearrange("r (g n) -> r g n", g=PASSES),
                x_scales[:, 4 * q : 4 * q + 4, :].bitcast(I32).rearrange("g r n -> r g n"),
            )
        raw0 = [load_w1(g, 0, 128, "raw0_%d" % g) for g in range(PASSES)]
        nc.sync.dma_start(xw[1][:].bitcast(I32), x_words[1].rearrange("p n t -> p (n t)").bitcast(I32))
        nc.sync.dma_start(cell_t[:], cell)
        raw1 = [load_w1(g, 128, 256, "raw1_%d" % g) for g in range(PASSES)]
        raw23 = [load_w1(g, 256, 512, "raw23_%d" % g) for g in range(PASSES)]
        skip_t = [sb.tile([P, U], F32, name="skip%d" % b) for b in range(4)]
        skip_dealt = skip[256:512, :].rearrange("(r u e) v -> u r e v", u=2, e=2)
        skip_rows = [skip[0:128, :], skip[128:256, :], skip_dealt[0], skip_dealt[1]]
        for b in range(4):
            nc.sync.dma_start(skip_t[b][:], skip_rows[b])

        ident = sb.tile([P, P], F32, name="ident")
        make_identity(nc, ident[:])
        w2c = sb.tile([P, 2 * N], U8, name="w2c", align_bytes=64)
        nc.sync.dma_start(w2c[:].bitcast(I32), w2_words[0].bitcast(I32))
        w2s = sb.tile([P, N], U8, name="w2s", align_bytes=64)
        nc.gpsimd.memset(w2s[:], 0)
        for q in range(4):
            nc.sync.dma_start(w2s[32 * q : 32 * q + 4, :].bitcast(I32), w2_scales[0, 4 * q : 4 * q + 4, :].bitcast(I32))

        up = [sb.tile([P, U], F32, name="up%d" % b, tag="up%d" % b) for b in range(4)]
        for b in range(2):
            nc.vector.memset(up[b][:], 0.0)
            nc.scalar.activation(up[b + 2][:], up[b][:], COPY)

        def quantise(grouped, width, name):
            codes = sb.tile([P, width], U32, name=name + "_c", align_bytes=64)
            scales = sb.tile([P, width], U8, name=name + "_s", align_bytes=64)
            nc.vector.quantize_mx(out=codes[:].bitcast(FP8X4), scales=scales[:], in_=grouped)
            return codes, scales

        def w1_plain(raw, name):
            grouped = sb.tile([P, PASSES, K_PASS], BF16, name=name, align_bytes=64)
            for g in range(PASSES):
                nc.scalar.activation(
                    grouped[:, g, :].rearrange("p (c i t) -> p c t i", i=4, t=PACK),
                    raw[g][:].rearrange("p t (c i) -> p c t i", i=4),
                    COPY,
                )
            return quantise(grouped[:].rearrange("p g n -> p (g n)"), PASSES * P, name)

        def w1_dealt(raw, name):
            grouped = sb.tile([P, 2, PASSES, K_PASS], BF16, name=name, align_bytes=64)
            for g in range(PASSES):
                nc.scalar.copy(
                    grouped[:, :, g, :].rearrange("p u (r e j) -> p r j u e", e=2, j=PACK),
                    raw[g][:].rearrange("p j (r u e) -> p r j u e", u=2, e=2),
                )
            return [quantise(grouped[:, u].rearrange("p g n -> p (g n)"), PASSES * P, "%s_%d" % (name, u)) for u in range(2)]

        w0 = w1_plain(raw0, "w0")

        xsg = [sb.tile([P, S], U8, name="xsg%d" % g, align_bytes=64) for g in range(PASSES)]
        for g in range(PASSES):
            nc.vector.tensor_copy(xsg[g][:], xs[:, g * T : (g + 1) * T].indirect(offs_t[:]))
        xg0 = sb.tile([P, S], U32, name="xg0", align_bytes=64)
        nc.vector.tensor_copy(xg0[:], xw[0][:].indirect(offs_t[:]))
        xg1_first = sb.tile([P, FIRST], U32, name="xg1_first", align_bytes=64)
        nc.vector.tensor_copy(xg1_first[:], xw[1][:].indirect(offs_t[:, 0 : FIRST // 16]))
        xg1_rest = sb.tile([P, S - FIRST], U32, name="xg1_rest", align_bytes=64)
        nc.vector.tensor_copy(xg1_rest[:], xw[1][:].indirect(offs_t[:, FIRST // 16 : S // 16]))

        def first_product(acc, j0, j1, w, col0):
            codes, scales = w
            cols = slice(j0, j1)
            moving = [xg0[:, cols], xg1_first[:] if j0 == 0 else xg1_rest[:, j0 - FIRST : j1 - FIRST]]
            for g in range(PASSES):
                wc = slice(col0 + g * P, col0 + (g + 1) * P)
                nc.tensor.matmul_mx(
                    out=acc,
                    lhsT=codes[:, wc].bitcast(FP8X4),
                    lhsT_scale=scales[:, wc],
                    rhs=moving[g].bitcast(FP8X4),
                    rhs_scale=xsg[g][:, cols],
                    start=(g == 0),
                    stop=(g == PASSES - 1),
                )

        def half_product(b, s, w, col0):
            acc = bank((0, 4, 0, 2)[b] + s, [P, HALF], "h%d_%d" % (b, s))
            first_product(acc[:], s * HALF, (s + 1) * HALF, w, col0)
            return acc

        def scatter(b, values, j0, j1):
            nc.vector.tensor_copy(up[b][:].indirect(cell_t[:, j0 // 16 : j1 // 16]), values)

        def relu_scatter(b, j0, j1, acc, tag):
            hs = sb.tile([P, j1 - j0], F32, name="hs%d_%d" % (b, j0), tag=tag)
            nc.scalar.activation(hs[:], acc[:], RELU)
            scatter(b, hs[:], j0, j1)

        def whole_tile(b, w):
            hs = sb.tile([P, S], F32, name="hs%d" % b)
            for s in range(2):
                nc.scalar.activation(hs[:, s * HALF : (s + 1) * HALF], w[s][:], RELU)
            scatter(b, hs[:], 0, S)

        zt0 = [sb.tile([P, 4, 256], BF16, name="zt0_%d" % vg, tag="zt0_%d" % vg) for vg in range(2)]
        zt1 = [sb.tile([P, 2, 256], BF16, name="zt1_%d" % q) for q in range(4)]

        def turn_and_add(b, number, vb0, count, ident_up):
            acc = bank(number, [P, count, P], "t%d_%d" % (b, vb0))
            for n, (src, one) in enumerate(((skip_t[b], ident), (up[b], ident_up))):
                for vb in range(count):
                    v0 = (vb0 + vb) * P
                    nc.tensor.matmul(acc[:, vb, :], src[:, v0 : v0 + P], one[:], start=(n == 0 and vb == 0), stop=(n == 1 and vb == count - 1), is_transpose=True)
            return acc

        def round_plain(b, banks):
            for vg in range(2):
                src = turn_and_add(b, banks[vg], 4 * vg, 4, ident)[:].rearrange("p vb (r u e) -> p u vb r e", u=2, e=2)
                nc.scalar.copy(zt0[vg][:, :, 64 * b : 64 * (b + 1)].rearrange("p vb (r e) -> p vb r e", e=2), src[:, 0])
                for h in range(2):
                    nc.scalar.copy(zt1[2 * vg + h][:, :, 64 * b : 64 * (b + 1)].rearrange("p vb (r e) -> p vb r e", e=2), src[:, 1, 2 * h : 2 * h + 2])

        def turn_back(u, q, view):
            for vb in range(2):
                nc.tensor.transpose(words[q][:, u, vb * P : (vb + 1) * P], view[:, vb, :], ident[:])

        relu_scatter(0, 0, HALF, half_product(0, 0, w0, 0), "hs0_0")
        acc = half_product(0, 1, w0, 0)
        w1q = w1_plain(raw1, "w1q")
        relu_scatter(0, HALF, S, acc, "raw1_1")
        relu_scatter(1, 0, HALF, half_product(1, 0, w1q, 0), "hs1_0")
        acc = half_product(1, 1, w1q, 0)
        w23 = w1_dealt(raw23, "w23")
        relu_scatter(1, HALF, S, acc, "raw23_1")
        late = [[half_product(2 + u, s, w23[u], 0) for s in range(2)] for u in range(2)]
        whole_tile(2, late[0])
        whole_tile(3, late[1])

        round_plain(1, (0, 1))
        round_plain(0, (4, 3))
        for vg in range(2):
            nc.scalar.copy(zt0[vg][:, :, 128:256], turn_and_add(2, 6 + vg, 4 * vg, 4, ident)[:])
        words = [bank(4 + q, [P, 2, QUARTER], "words%d" % q) for q in range(4)]
        for q in range(4):
            turn_back(0, q, zt0[q // 2][:].bitcast(F32)[:, 2 * (q % 2) : 2 * (q % 2) + 2, :])

        ident_last = sb.tile([P, P], F32, name="ident_last", tag="zt0_0")
        nc.scalar.copy(ident_last[:], ident[:])
        for q in range(4):
            (nc.vector.tensor_copy, nc.scalar.copy)[q % 2](zt1[q][:, :, 128:256], turn_and_add(3, q, 2 * q, 2, ident_last)[:])
        for q in range(4):
            turn_back(1, q, zt1[q][:].bitcast(F32))

        zb = [sb.tile([P, QUARTER * PACK], BF16, name="zb%d" % q, align_bytes=64) for q in range(4)]
        weave = [nc.scalar.copy, nc.vector.tensor_copy, nc.scalar.copy, nc.scalar.copy]
        for q in range(4):
            weave[q](zb[q][:].bitcast(F32).rearrange("p (v u) -> p v u", u=2), words[q][:].rearrange("p u v -> p v u"))
        leave = [nc.scalar.copy, nc.scalar.copy, nc.scalar.copy, nc.vector.tensor_copy]
        for q in range(4):
            codes, scales = quantise(zb[q][:], QUARTER, "zq%d" % q)
            acc = bank(q, [P, QUARTER], "o%d" % q)
            nc.tensor.matmul_mx(
                out=acc[:],
                lhsT=w2c[:].bitcast(FP4X4),
                lhsT_scale=w2s[:],
                rhs=codes[:].bitcast(FP8X4),
                rhs_scale=scales[:],
                start=True,
                stop=True,
            )
            res = sb.tile([P, QUARTER], F32, name="res%d" % q)
            leave[q](res[:], acc[:])
            nc.sync.dma_start(out[:, q * QUARTER : (q + 1) * QUARTER], res[:])
